import numpy as np
import ml_dtypes


def mxq(x, axis, fmt="e4m3"):
    dtype, down = {"e4m3": (ml_dtypes.float8_e4m3fn, 7), "e5m2": (ml_dtypes.float8_e5m2, 14)}[fmt]
    v = np.moveaxis(np.asarray(x, np.float32).astype(ml_dtypes.bfloat16).astype(np.float64), axis, -1)
    blocks = v.reshape(v.shape[:-1] + (-1, 32))
    amax = np.abs(blocks).max(-1, keepdims=True)
    byte = np.maximum(np.where(amax > 0, np.frexp(amax)[1] - 1 + 127, 0) - down, 1)
    scale = np.exp2(byte - 127.0)
    codes = (blocks / scale).astype(np.float32).astype(dtype).astype(np.float64)
    return np.moveaxis((codes * scale).reshape(v.shape), -1, axis)


WIDE = False


def mx_kscale(k):
    if not WIDE:
        return np.ones(k)
    levels = np.array([10, -10, 5, -5, 0])
    if k % 512:
        return np.exp2(np.random.permutation(np.resize(levels, k // 32))).repeat(32)
    a = np.empty((k // 512, 16))
    for p in range(k // 512):
        a[p, :8] = np.random.permutation(np.resize(levels, 8))
        for g in range(8):
            far = levels[np.abs(levels - a[p, g]) >= 10]
            a[p, g + 8] = far[np.random.randint(len(far))]
    return np.exp2(a.ravel()).repeat(32)


def f64(x):
    return np.asarray(x).astype(np.float64)


def striped(idx):
    return np.tile(idx.reshape(-1, 16).T, (8, 1)).astype(np.uint16)


def unstriped(offs):
    return offs[:16].T.reshape(-1).astype(np.int64)


def relu2(v):
    return np.maximum(v, 0.0) ** 2


K, T, E, C, H, N = 512, 512, 8, 256, 512, 256
TOP = 4


def by_expert(wq, xq):
    return np.concatenate([wq[e].T @ xq[:, e * C:(e + 1) * C] for e in range(E)], axis=1)


def setup_inputs():
    n = np.random.standard_normal
    s = mx_kscale(K)[:, None]
    u = mx_kscale(H)
    deal = np.repeat(np.arange(E), C).reshape(TOP, T)[:, np.random.permutation(T)]
    deal = np.take_along_axis(deal, np.argsort(np.random.rand(TOP, T), axis=0), axis=0)
    for _ in range(8):
        s_, t_ = np.random.permutation(T).reshape(2, -1); r = np.random.randint(TOP, size=T // 2); x, y = deal[r, s_].copy(), deal[r, t_].copy()
        ok = ~((deal[:, s_] == y).any(0) | (deal[:, t_] == x).any(0)); deal[r[ok], s_[ok]] = y[ok]; deal[r[ok], t_[ok]] = x[ok]
    order = np.lexsort((np.random.rand(TOP * T), deal.reshape(-1)))
    slot_token = order % T; pos = np.empty(TOP * T, np.int64); pos[order] = np.arange(TOP * T); pos = pos.reshape(TOP, T)
    g = np.random.uniform(0.5, 1.5, (TOP, T)); g = g / g.sum(0)
    return {
        "xT": (n((K, T)) * s).astype(np.float32),
        "w1": (n((E, K, H)) / np.sqrt(K) / s[None] * u[None, None, :]).astype(np.float32),
        "w2": (n((E, H, N)) / np.sqrt(H) / u[None, :, None] ** 2).astype(np.float32),
        "gate": np.stack([np.tile(r, (N, 1)) for r in g]).astype(np.float32),
        "offs": striped(slot_token),
        "pos1": striped(pos[0]),
        "pos2": striped(pos[1]),
        "pos3": striped(pos[2]),
        "pos4": striped(pos[3]),
    }


def reference(xT, w1, w2, gate, offs, pos1, pos2, pos3, pos4):
    idx = unstriped(offs)
    xq = mxq(f64(xT)[:, idx], 0, "e4m3")
    h = relu2(by_expert(mxq(f64(w1), 1, "e4m3"), xq))
    y = by_expert(mxq(f64(w2), 1, "e4m3"), mxq(h, 0, "e4m3"))
    return sum(f64(gate[r]) * y[:, unstriped(p)] for r, p in enumerate((pos1, pos2, pos3, pos4)))

@@ -1,0 +1,177 @@
+from contextlib import ExitStack
+
+import concourse.mybir as mybir
+
+K, T, E, C, H, N = 512, 512, 8, 256, 512, 256
+TOP = 4
+P = 128
+PACK = 4
+FLOPS = 2 * E * C * (K * H + H * N)
+
+F32 = mybir.dt.float32
+BF16 = mybir.dt.bfloat16
+U32 = mybir.dt.uint32
+U16 = mybir.dt.uint16
+U8 = mybir.dt.uint8
+FP8X4 = mybir.dt.float8_e4m3fn_x4
+MULT = mybir.AluOpType.mult
+ADD = mybir.AluOpType.add
+RELU = mybir.ActivationFunctionType.Relu
+SQUARE = mybir.ActivationFunctionType.Square
+
+W1_VECTOR = (0, 32, 128, 96, 96, 96, 128, 96)
+SQUARE_ON_VECTOR = (7,)
+W2_ON_VECTOR = {0: (0, 2, 4, 6), 1: (0, 1, 2, 4, 5)}
+
+
+def tile_moe_tk_mlp_relu2_kernel(tc, xT, w1, w2, gate, offs, pos1, pos2, pos3, pos4, out):
+    nc = tc.nc
+    pos = (pos1, pos2, pos3, pos4)
+    with ExitStack() as ctx:
+        keep = ctx.enter_context(tc.tile_pool(name="keep", bufs=1))
+        stage = ctx.enter_context(tc.tile_pool(name="stage", bufs=2))
+        slots_pool = ctx.enter_context(tc.tile_pool(name="slots", bufs=3))
+        sums = ctx.enter_context(tc.tile_pool(name="sums", bufs=1))
+        codes = ctx.enter_context(tc.tile_pool(name="codes", bufs=3))
+        psum1 = ctx.enter_context(tc.psum_pool(name="psum1", bufs=4))
+        psum2 = ctx.enter_context(tc.psum_pool(name="psum2", bufs=4))
+
+        xs = keep.tile([P, T], U8, name="xs", align_bytes=64)
+        nc.gpsimd.memset(xs[:], 0)
+        x_view = xT.rearrange("(p j) t -> p j t", j=PACK)
+        x_raw = []
+        for c in range(2):
+            t_ = keep.tile([P, PACK, T // 2], F32, name=f"x_raw{c}", align_bytes=64)
+            nc.sync.dma_start(out=t_[:], in_=x_view[:, :, c * (T // 2) : (c + 1) * (T // 2)])
+            x_raw.append(t_)
+        offs_t = keep.tile([P, E * C // 16], U16, name="offs_t")
+        nc.sync.dma_start(offs_t[:], offs)
+        w1_raw = []
+        for e in range(E):
+            t_ = keep.tile([P, PACK, H], F32, name=f"w1_raw{e}", align_bytes=64)
+            nc.sync.dma_start(out=t_[:], in_=w1[e].rearrange("(p j) c -> p j c", j=PACK))
+            w1_raw.append(t_)
+        w2_raw = []
+        for e in range(E):
+            t_ = keep.tile([P, PACK, N], F32, name=f"w2_raw{e}", align_bytes=64)
+            nc.sync.dma_start(out=t_[:], in_=w2[e].rearrange("(p j) n -> p j n", j=PACK))
+            w2_raw.append(t_)
+        pos_t = []
+        for r in range(TOP):
+            t_ = keep.tile([P, T // 16], U16, name=f"pos_t{r}")
+            nc.sync.dma_start(t_[:], pos[r])
+            pos_t.append(t_)
+        gates = []
+        for h in range(2):
+            t_ = keep.tile([P, TOP, T], F32, name=f"gates{h}", align_bytes=64)
+            nc.sync.dma_start(out=t_[:], in_=gate[:, h * P : (h + 1) * P, :].rearrange("r p t -> p r t"))
+            gates.append(t_)
+
+        xw = keep.tile([P, T], U32, name="xw", align_bytes=64)
+        for c in range(2):
+            xg = keep.tile([P, T // 2, PACK], BF16, name=f"xg{c}", align_bytes=64)
+            nc.vector.tensor_copy(
+                out=xg[:].rearrange("p (c i) j -> p c j i", i=4),
+                in_=x_raw[c][:].rearrange("p j (c i) -> p c j i", i=4),
+            )
+            cols = slice(c * (T // 2), (c + 1) * (T // 2))
+            nc.vector.quantize_mx(out=xw[:, cols].bitcast(FP8X4), scales=xs[:, cols], in_=xg[:].rearrange("p c j -> p (c j)"))
+
+        hc, hs = [], []
+
+        def w1_copy(e):
+            g = stage.tile([P, PACK * H], BF16, name="w1_grouped", align_bytes=64)
+            dst = g[:].rearrange("p (t m j) -> p m j t", t=4, j=PACK)
+            src = w1_raw[e][:].rearrange("p j (m t) -> p m j t", t=4)
+            v = W1_VECTOR[e]
+            if v < P:
+                nc.scalar.copy(out=dst[:, v:], in_=src[:, v:])
+            if v > 0:
+                nc.vector.tensor_copy(out=dst[:, :v], in_=src[:, :v])
+            return g
+
+        def expert_first(e):
+            g = w1_copy(e)
+            slots = slice(e * (C // 16), (e + 1) * (C // 16))
+            xe = slots_pool.tile([P, C], U32, name="xe", align_bytes=64)
+            xse = slots_pool.tile([P, C], U8, name="xse", align_bytes=64)
+            nc.vector.tensor_copy(xe[:], xw[:].indirect(offs_t[:, slots]))
+            nc.vector.tensor_copy(xse[:], xs[:].indirect(offs_t[:, slots]))
+            wc = codes.tile([P, H], U32, name="w1_codes", align_bytes=64)
+            ws = codes.tile([P, H], U8, name="w1_scales", align_bytes=64)
+            nc.vector.quantize_mx(out=wc[:].bitcast(FP8X4), scales=ws[:], in_=g[:])
+            pos_part = stage.tile([P, C, PACK], F32, name="pos_part", align_bytes=64)
+            for b in range(2):
+                ps = psum1.tile([P, PACK, P], F32, name="ps1")
+                cols = slice(b * P, (b + 1) * P)
+                for t in range(PACK):
+                    m = slice(t * P, (t + 1) * P)
+                    nc.tensor.matmul_mx(
+                        out=ps[:, t, :], lhsT=wc[:, m].bitcast(FP8X4), lhsT_scale=ws[:, m],
+                        rhs=xe[:, cols].bitcast(FP8X4), rhs_scale=xse[:, cols], start=True, stop=True,
+                    )
+                nc.scalar.activation(pos_part[:, cols, :], ps[:].rearrange("p t n -> p n t"), RELU)
+            hb = stage.tile([P, C * PACK], BF16, name="hb", align_bytes=64)
+            flat = pos_part[:].rearrange("p n t -> p (n t)")
+            if e in SQUARE_ON_VECTOR:
+                nc.vector.tensor_tensor(hb[:], flat, flat, MULT)
+            else:
+                nc.scalar.activation(hb[:], flat, SQUARE)
+            c_ = keep.tile([P, C], U32, name=f"h_codes{e}", align_bytes=64)
+            s_ = keep.tile([P, C], U8, name=f"h_scales{e}", align_bytes=64)
+            nc.vector.quantize_mx(out=c_[:].bitcast(FP8X4), scales=s_[:], in_=hb[:])
+            hc.append(c_)
+            hs.append(s_)
+
+        y = [keep.tile([P, E * C], F32, name=f"y{h}") for h in range(2)]
+
+        def pair_second(q, h):
+            g = stage.tile([P, 2, P, PACK], BF16, name="w2_grouped", align_bytes=64)
+            for i in range(2):
+                e = 2 * q + i
+                dst = g[:, i].rearrange("p (c i) j -> p c j i", i=4)
+                src = w2_raw[e][:, :, h * P : (h + 1) * P].rearrange("p j (c i) -> p c j i", i=4)
+                if e in W2_ON_VECTOR[h]:
+                    nc.vector.tensor_copy(out=dst, in_=src)
+                else:
+                    nc.scalar.copy(out=dst, in_=src)
+            wc = codes.tile([P, 2 * P], U32, name="w2_codes", align_bytes=64)
+            ws = codes.tile([P, 2 * P], U8, name="w2_scales", align_bytes=64)
+            nc.vector.quantize_mx(out=wc[:].bitcast(FP8X4), scales=ws[:], in_=g[:].rearrange("p i c j -> p (i c j)"))
+            ps = psum2.tile([P, 2, C], F32, name="ps2")
+            for i in range(2):
+                e = 2 * q + i
+                m = slice(i * P, (i + 1) * P)
+                nc.tensor.matmul_mx(
+                    out=ps[:, i, :], lhsT=wc[:, m].bitcast(FP8X4), lhsT_scale=ws[:, m],
+                    rhs=hc[e][:].bitcast(FP8X4), rhs_scale=hs[e][:], start=True, stop=True,
+                )
+            nc.scalar.copy(out=y[h][:, 2 * q * C : (2 * q + 2) * C], in_=ps[:].rearrange("p i c -> p (i c)"))
+
+        def combine(h):
+            prod = [sums.tile([P, T], F32, name=f"prod{r}") for r in range(TOP)]
+
+            def fetch(r):
+                nc.vector.tensor_tensor(prod[r][:], y[h][:].indirect(pos_t[r][:]), gates[h][:, r, :], MULT)
+
+            s01 = sums.tile([P, T], F32, name="s01")
+            s012 = sums.tile([P, T], F32, name="s012")
+            res = sums.tile([P, T], F32, name="res")
+            fetch(0)
+            fetch(1)
+            fetch(2)
+            nc.vector.tensor_tensor(s01[:], prod[0][:], prod[1][:], ADD)
+            fetch(3)
+            nc.vector.tensor_tensor(s012[:], s01[:], prod[2][:], ADD)
+            for c in range(2):
+                cols = slice(c * (T // 2), (c + 1) * (T // 2))
+                nc.vector.tensor_tensor(res[:, cols], s012[:, cols], prod[3][:, cols], ADD)
+                nc.sync.dma_start(out[h * P : (h + 1) * P, cols], res[:, cols])
+
+        for e in range(E):
+            expert_first(e)
+        for h in range(2):
+            for q in range(E // 2):
+                pair_second(q, h)
+        for h in range(2):
+            combine(h)

@@ -19,9 +19,10 @@ ADD = mybir.AluOpType.add
 RELU = mybir.ActivationFunctionType.Relu
 SQUARE = mybir.ActivationFunctionType.Square
 
-W1_VECTOR = (0, 32, 128, 96, 96, 96, 128, 96)
-SQUARE_ON_VECTOR = (7,)
-W2_ON_VECTOR = {0: (0, 2, 4, 6), 1: (0, 1, 2, 4, 5)}
+W1_VECTOR = (0, 48, 128, 128, 128, 0, 112, 128)
+SQUARE_ON_VECTOR = (6,)
+W2_ON_VECTOR = ((0, 0), (0, 2), (0, 3), (1, 0), (1, 1),)
+PIECE = 384
 
 
 def tile_moe_tk_mlp_relu2_kernel(tc, xT, w1, w2, gate, offs, pos1, pos2, pos3, pos4, out):
@@ -30,7 +31,8 @@ def tile_moe_tk_mlp_relu2_kernel(tc, xT, w1, w2, gate, offs, pos1, pos2, pos3, p
     with ExitStack() as ctx:
         keep = ctx.enter_context(tc.tile_pool(name="keep", bufs=1))
         stage = ctx.enter_context(tc.tile_pool(name="stage", bufs=2))
-        slots_pool = ctx.enter_context(tc.tile_pool(name="slots", bufs=3))
+        grouped = ctx.enter_context(tc.tile_pool(name="grouped", bufs=3))
+        slots_pool = ctx.enter_context(tc.tile_pool(name="slots", bufs=2))
         sums = ctx.enter_context(tc.tile_pool(name="sums", bufs=1))
         codes = ctx.enter_context(tc.tile_pool(name="codes", bufs=3))
         psum1 = ctx.enter_context(tc.psum_pool(name="psum1", bufs=4))
@@ -48,13 +50,18 @@ def tile_moe_tk_mlp_relu2_kernel(tc, xT, w1, w2, gate, offs, pos1, pos2, pos3, p
         nc.sync.dma_start(offs_t[:], offs)
         w1_raw = []
         for e in range(E):
-            t_ = keep.tile([P, PACK, H], F32, name=f"w1_raw{e}", align_bytes=64)
-            nc.sync.dma_start(out=t_[:], in_=w1[e].rearrange("(p j) c -> p j c", j=PACK))
-            w1_raw.append(t_)
+            n_parts = 2 if e == 0 else 1
+            parts = []
+            for i in range(n_parts):
+                width = H // n_parts
+                t_ = keep.tile([P, PACK, width], F32, name=f"w1_raw{e}_{i}", align_bytes=64)
+                nc.sync.dma_start(out=t_[:], in_=w1[e].rearrange("(p j) c -> p j c", j=PACK)[:, :, i * width : (i + 1) * width])
+                parts.append(t_)
+            w1_raw.append(parts)
         w2_raw = []
-        for e in range(E):
-            t_ = keep.tile([P, PACK, N], F32, name=f"w2_raw{e}", align_bytes=64)
-            nc.sync.dma_start(out=t_[:], in_=w2[e].rearrange("(p j) n -> p j n", j=PACK))
+        for q in range(E // 2):
+            t_ = keep.tile([P, 2, PACK, N], F32, name=f"w2_raw{q}", align_bytes=64)
+            nc.sync.dma_start(out=t_[:], in_=w2[2 * q : 2 * q + 2].rearrange("i (p j) n -> p i j n", j=PACK))
             w2_raw.append(t_)
         pos_t = []
         for r in range(TOP):
@@ -77,12 +84,17 @@ def tile_moe_tk_mlp_relu2_kernel(tc, xT, w1, w2, gate, offs, pos1, pos2, pos3, p
             cols = slice(c * (T // 2), (c + 1) * (T // 2))
             nc.vector.quantize_mx(out=xw[:, cols].bitcast(FP8X4), scales=xs[:, cols], in_=xg[:].rearrange("p c j -> p (c j)"))
 
-        hc, hs = [], []
+        hb_pair, h_codes, h_scales, pieces = [], [], [], []
 
         def w1_copy(e):
-            g = stage.tile([P, PACK * H], BF16, name="w1_grouped", align_bytes=64)
+            g = grouped.tile([P, PACK * H], BF16, name="w1_grouped", align_bytes=64)
             dst = g[:].rearrange("p (t m j) -> p m j t", t=4, j=PACK)
-            src = w1_raw[e][:].rearrange("p j (m t) -> p m j t", t=4)
+            if e == 0:
+                a0, a1 = [t_[:].rearrange("p j (m t) -> p m j t", t=4) for t_ in w1_raw[e]]
+                nc.scalar.copy(out=dst[:, : P // 2], in_=a0)
+                nc.scalar.copy(out=dst[:, P // 2 :], in_=a1)
+                return g
+            src = w1_raw[e][0][:].rearrange("p j (m t) -> p m j t", t=4)
             v = W1_VECTOR[e]
             if v < P:
                 nc.scalar.copy(out=dst[:, v:], in_=src[:, v:])
@@ -92,11 +104,15 @@ def tile_moe_tk_mlp_relu2_kernel(tc, xT, w1, w2, gate, offs, pos1, pos2, pos3, p
 
         def expert_first(e):
             g = w1_copy(e)
-            slots = slice(e * (C // 16), (e + 1) * (C // 16))
-            xe = slots_pool.tile([P, C], U32, name="xe", align_bytes=64)
-            xse = slots_pool.tile([P, C], U8, name="xse", align_bytes=64)
-            nc.vector.tensor_copy(xe[:], xw[:].indirect(offs_t[:, slots]))
-            nc.vector.tensor_copy(xse[:], xs[:].indirect(offs_t[:, slots]))
+            while len(pieces) * PIECE < (e + 1) * C:
+                s0 = len(pieces) * PIECE
+                s1 = min(s0 + PIECE, E * C)
+                xe = slots_pool.tile([P, PIECE], U32, name="xe", align_bytes=64)
+                xse = slots_pool.tile([P, PIECE], U8, name="xse", align_bytes=64)
+                lst = offs_t[:, s0 // 16 : s1 // 16]
+                nc.vector.tensor_copy(xe[:, : s1 - s0], xw[:].indirect(lst))
+                nc.vector.tensor_copy(xse[:, : s1 - s0], xs[:].indirect(lst))
+                pieces.append((xe, xse))
             wc = codes.tile([P, H], U32, name="w1_codes", align_bytes=64)
             ws = codes.tile([P, H], U8, name="w1_scales", align_bytes=64)
             nc.vector.quantize_mx(out=wc[:].bitcast(FP8X4), scales=ws[:], in_=g[:])
@@ -104,74 +120,90 @@ def tile_moe_tk_mlp_relu2_kernel(tc, xT, w1, w2, gate, offs, pos1, pos2, pos3, p
             for b in range(2):
                 ps = psum1.tile([P, PACK, P], F32, name="ps1")
                 cols = slice(b * P, (b + 1) * P)
+                s0 = e * C + b * P
+                xe, xse = pieces[s0 // PIECE]
+                part = slice(s0 % PIECE, s0 % PIECE + P)
                 for t in range(PACK):
                     m = slice(t * P, (t + 1) * P)
                     nc.tensor.matmul_mx(
                         out=ps[:, t, :], lhsT=wc[:, m].bitcast(FP8X4), lhsT_scale=ws[:, m],
-                        rhs=xe[:, cols].bitcast(FP8X4), rhs_scale=xse[:, cols], start=True, stop=True,
+                        rhs=xe[:, part].bitcast(FP8X4), rhs_scale=xse[:, part], start=True, stop=True,
                     )
                 nc.scalar.activation(pos_part[:, cols, :], ps[:].rearrange("p t n -> p n t"), RELU)
-            hb = stage.tile([P, C * PACK], BF16, name="hb", align_bytes=64)
+            if e % 2 == 0:
+                hb_pair.append(stage.tile([P, 2 * C * PACK], BF16, name="hb", align_bytes=64))
+                h_codes.append(keep.tile([P, 2 * C], U32, name=f"h_codes{e}", align_bytes=64))
+                h_scales.append(keep.tile([P, 2 * C], U8, name=f"h_scales{e}", align_bytes=64))
+            i = e % 2
+            hb = hb_pair[-1][:, i * C * PACK : (i + 1) * C * PACK]
             flat = pos_part[:].rearrange("p n t -> p (n t)")
             if e in SQUARE_ON_VECTOR:
-                nc.vector.tensor_tensor(hb[:], flat, flat, MULT)
+                nc.vector.tensor_tensor(hb, flat, flat, MULT)
             else:
-                nc.scalar.activation(hb[:], flat, SQUARE)
-            c_ = keep.tile([P, C], U32, name=f"h_codes{e}", align_bytes=64)
-            s_ = keep.tile([P, C], U8, name=f"h_scales{e}", align_bytes=64)
-            nc.vector.quantize_mx(out=c_[:].bitcast(FP8X4), scales=s_[:], in_=hb[:])
-            hc.append(c_)
-            hs.append(s_)
+                nc.scalar.activation(hb, flat, SQUARE)
+            if e in (0, 1, 6, 7,):
+                cols, src = slice(i * C, (i + 1) * C), hb
+            elif i == 1:
+                cols, src = slice(0, 2 * C), hb_pair[-1][:]
+            else:
+                return
+            nc.vector.quantize_mx(out=h_codes[-1][:, cols].bitcast(FP8X4), scales=h_scales[-1][:, cols], in_=src)
 
         y = [keep.tile([P, E * C], F32, name=f"y{h}") for h in range(2)]
 
         def pair_second(q, h):
             g = stage.tile([P, 2, P, PACK], BF16, name="w2_grouped", align_bytes=64)
-            for i in range(2):
-                e = 2 * q + i
-                dst = g[:, i].rearrange("p (c i) j -> p c j i", i=4)
-                src = w2_raw[e][:, :, h * P : (h + 1) * P].rearrange("p j (c i) -> p c j i", i=4)
-                if e in W2_ON_VECTOR[h]:
-                    nc.vector.tensor_copy(out=dst, in_=src)
-                else:
-                    nc.scalar.copy(out=dst, in_=src)
+            dst = g[:].rearrange("p e (c i) j -> p e c j i", i=4)
+            src = w2_raw[q][:, :, :, h * P : (h + 1) * P].rearrange("p e j (c i) -> p e c j i", i=4)
+            if (h, q) in W2_ON_VECTOR:
+                nc.vector.tensor_copy(out=dst, in_=src)
+            else:
+                nc.scalar.copy(out=dst, in_=src)
             wc = codes.tile([P, 2 * P], U32, name="w2_codes", align_bytes=64)
             ws = codes.tile([P, 2 * P], U8, name="w2_scales", align_bytes=64)
             nc.vector.quantize_mx(out=wc[:].bitcast(FP8X4), scales=ws[:], in_=g[:].rearrange("p i c j -> p (i c j)"))
             ps = psum2.tile([P, 2, C], F32, name="ps2")
             for i in range(2):
-                e = 2 * q + i
                 m = slice(i * P, (i + 1) * P)
+                cols = slice(i * C, (i + 1) * C)
                 nc.tensor.matmul_mx(
                     out=ps[:, i, :], lhsT=wc[:, m].bitcast(FP8X4), lhsT_scale=ws[:, m],
-                    rhs=hc[e][:].bitcast(FP8X4), rhs_scale=hs[e][:], start=True, stop=True,
+                    rhs=h_codes[q][:, cols].bitcast(FP8X4), rhs_scale=h_scales[q][:, cols], start=True, stop=True,
                 )
             nc.scalar.copy(out=y[h][:, 2 * q * C : (2 * q + 2) * C], in_=ps[:].rearrange("p i c -> p (i c)"))
 
         def combine(h):
             prod = [sums.tile([P, T], F32, name=f"prod{r}") for r in range(TOP)]
 
-            def fetch(r):
-                nc.vector.tensor_tensor(prod[r][:], y[h][:].indirect(pos_t[r][:]), gates[h][:, r, :], MULT)
+            def fetch(r, t0, t1):
+                nc.vector.tensor_tensor(
+                    prod[r][:, t0:t1], y[h][:].indirect(pos_t[r][:, t0 // 16 : t1 // 16]), gates[h][:, r, t0:t1], MULT
+                )
 
             s01 = sums.tile([P, T], F32, name="s01")
             s012 = sums.tile([P, T], F32, name="s012")
             res = sums.tile([P, T], F32, name="res")
-            fetch(0)
-            fetch(1)
-            fetch(2)
+            fetch(0, 0, T)
+            fetch(1, 0, T)
+            fetch(2, 0, T)
             nc.vector.tensor_tensor(s01[:], prod[0][:], prod[1][:], ADD)
-            fetch(3)
+            fetch(3, 0, T // 2)
             nc.vector.tensor_tensor(s012[:], s01[:], prod[2][:], ADD)
+            fetch(3, T // 2, T)
             for c in range(2):
                 cols = slice(c * (T // 2), (c + 1) * (T // 2))
                 nc.vector.tensor_tensor(res[:, cols], s012[:, cols], prod[3][:, cols], ADD)
                 nc.sync.dma_start(out[h * P : (h + 1) * P, cols], res[:, cols])
 
+        early = {0: 6, 1: 7, 2: 7}
         for e in range(E):
             expert_first(e)
+            for q in early:
+                if early[q] == e:
+                    pair_second(q, 0)
         for h in range(2):
             for q in range(E // 2):
-                pair_second(q, h)
+                if h == 1 or q not in early:
+                    pair_second(q, h)
         for h in range(2):
             combine(h)

@@ -78,8 +78,8 @@ def tile_moe_tk_mlp_relu2_kernel(tc, xT, w1, w2, gate, offs, pos1, pos2, pos3, p
         for c in range(2):
             xg = keep.tile([P, T // 2, PACK], BF16, name=f"xg{c}", align_bytes=64)
             nc.vector.tensor_copy(
-                out=xg[:].rearrange("p (c i) j -> p c j i", i=4),
-                in_=x_raw[c][:].rearrange("p j (c i) -> p c j i", i=4),
+                out=xg[:].rearrange("p (c i) j -> p c j i", i=2),
+                in_=x_raw[c][:].rearrange("p j (c i) -> p c j i", i=2),
             )
             cols = slice(c * (T // 2), (c + 1) * (T // 2))
             nc.vector.quantize_mx(out=xw[:, cols].bitcast(FP8X4), scales=xs[:, cols], in_=xg[:].rearrange("p c j -> p (c j)"))
@@ -153,8 +153,8 @@ def tile_moe_tk_mlp_relu2_kernel(tc, xT, w1, w2, gate, offs, pos1, pos2, pos3, p
 
         def pair_second(q, h):
             g = stage.tile([P, 2, P, PACK], BF16, name="w2_grouped", align_bytes=64)
-            dst = g[:].rearrange("p e (c i) j -> p e c j i", i=4)
-            src = w2_raw[q][:, :, :, h * P : (h + 1) * P].rearrange("p e j (c i) -> p e c j i", i=4)
+            dst = g[:].rearrange("p e (c i) j -> p e c j i", i=2)
+            src = w2_raw[q][:, :, :, h * P : (h + 1) * P].rearrange("p e j (c i) -> p e c j i", i=2)
             if (h, q) in W2_ON_VECTOR:
                 nc.vector.tensor_copy(out=dst, in_=src)
             else:
@@ -181,18 +181,16 @@ def tile_moe_tk_mlp_relu2_kernel(tc, xT, w1, w2, gate, offs, pos1, pos2, pos3, p
                 )
 
             s01 = sums.tile([P, T], F32, name="s01")
-            s012 = sums.tile([P, T], F32, name="s012")
+            s23 = sums.tile([P, T], F32, name="s23")
             res = sums.tile([P, T], F32, name="res")
-            fetch(0, 0, T)
-            fetch(1, 0, T)
-            fetch(2, 0, T)
+            for r in range(TOP):
+                fetch(r, 0, T)
             nc.vector.tensor_tensor(s01[:], prod[0][:], prod[1][:], ADD)
-            fetch(3, 0, T // 2)
-            nc.vector.tensor_tensor(s012[:], s01[:], prod[2][:], ADD)
-            fetch(3, T // 2, T)
-            for c in range(2):
-                cols = slice(c * (T // 2), (c + 1) * (T // 2))
-                nc.vector.tensor_tensor(res[:, cols], s012[:, cols], prod[3][:, cols], ADD)
+            halves = [slice(c * (T // 2), (c + 1) * (T // 2)) for c in range(2)]
+            for cols in halves:
+                nc.vector.tensor_tensor(s23[:, cols], prod[2][:, cols], prod[3][:, cols], ADD)
+            for cols in halves:
+                nc.vector.tensor_tensor(res[:, cols], s01[:, cols], s23[:, cols], ADD)
                 nc.sync.dma_start(out[h * P : (h + 1) * P, cols], res[:, cols])
 
         early = {0: 6, 1: 7, 2: 7}

@@ -20,7 +20,7 @@ RELU = mybir.ActivationFunctionType.Relu
 SQUARE = mybir.ActivationFunctionType.Square
 
 W1_VECTOR = (0, 48, 128, 128, 128, 0, 112, 128)
-SQUARE_ON_VECTOR = (6,)
+SQUARE_ON_VECTOR = ()
 W2_ON_VECTOR = ((0, 0), (0, 2), (0, 3), (1, 0), (1, 1),)
 PIECE = 384
 
@@ -33,6 +33,8 @@ def tile_moe_tk_mlp_relu2_kernel(tc, xT, w1, w2, gate, offs, pos1, pos2, pos3, p
         stage = ctx.enter_context(tc.tile_pool(name="stage", bufs=2))
         grouped = ctx.enter_context(tc.tile_pool(name="grouped", bufs=3))
         slots_pool = ctx.enter_context(tc.tile_pool(name="slots", bufs=2))
+        grouped2 = ctx.enter_context(tc.tile_pool(name="grouped2", bufs=4))
+        codes2 = ctx.enter_context(tc.tile_pool(name="codes2", bufs=5))
         sums = ctx.enter_context(tc.tile_pool(name="sums", bufs=1))
         codes = ctx.enter_context(tc.tile_pool(name="codes", bufs=3))
         psum1 = ctx.enter_context(tc.psum_pool(name="psum1", bufs=4))
@@ -84,7 +86,7 @@ def tile_moe_tk_mlp_relu2_kernel(tc, xT, w1, w2, gate, offs, pos1, pos2, pos3, p
             cols = slice(c * (T // 2), (c + 1) * (T // 2))
             nc.vector.quantize_mx(out=xw[:, cols].bitcast(FP8X4), scales=xs[:, cols], in_=xg[:].rearrange("p c j -> p (c j)"))
 
-        hb_pair, h_codes, h_scales, pieces = [], [], [], []
+        hb_pair, h_codes, h_scales, pieces, first = [], [], [], [], [0]
 
         def w1_copy(e):
             g = grouped.tile([P, PACK * H], BF16, name="w1_grouped", align_bytes=64)
@@ -130,21 +132,23 @@ def tile_moe_tk_mlp_relu2_kernel(tc, xT, w1, w2, gate, offs, pos1, pos2, pos3, p
                         rhs=xe[:, part].bitcast(FP8X4), rhs_scale=xse[:, part], start=True, stop=True,
                     )
                 nc.scalar.activation(pos_part[:, cols, :], ps[:].rearrange("p t n -> p n t"), RELU)
-            if e % 2 == 0:
-                hb_pair.append(stage.tile([P, 2 * C * PACK], BF16, name="hb", align_bytes=64))
-                h_codes.append(keep.tile([P, 2 * C], U32, name=f"h_codes{e}", align_bytes=64))
-                h_scales.append(keep.tile([P, 2 * C], U8, name=f"h_scales{e}", align_bytes=64))
-            i = e % 2
+            if e in (0, 4, 6):
+                n = 4 if e == 0 else 2
+                first[0] = e
+                hb_pair.append(keep.tile([P, n * C * PACK], BF16, name=f"hb{e}", align_bytes=64))
+                h_codes.append(keep.tile([P, n * C], U32, name=f"h_codes{e}", align_bytes=64))
+                h_scales.append(keep.tile([P, n * C], U8, name=f"h_scales{e}", align_bytes=64))
+            i = e - first[0]
             hb = hb_pair[-1][:, i * C * PACK : (i + 1) * C * PACK]
             flat = pos_part[:].rearrange("p n t -> p (n t)")
             if e in SQUARE_ON_VECTOR:
                 nc.vector.tensor_tensor(hb, flat, flat, MULT)
             else:
                 nc.scalar.activation(hb, flat, SQUARE)
-            if e in (0, 1, 6, 7,):
+            if e >= 6:
                 cols, src = slice(i * C, (i + 1) * C), hb
-            elif i == 1:
-                cols, src = slice(0, 2 * C), hb_pair[-1][:]
+            elif e in (3, 5):
+                cols, src = slice(0, (i + 1) * C), hb_pair[-1][:]
             else:
                 return
             nc.vector.quantize_mx(out=h_codes[-1][:, cols].bitcast(FP8X4), scales=h_scales[-1][:, cols], in_=src)
@@ -152,23 +156,26 @@ def tile_moe_tk_mlp_relu2_kernel(tc, xT, w1, w2, gate, offs, pos1, pos2, pos3, p
         y = [keep.tile([P, E * C], F32, name=f"y{h}") for h in range(2)]
 
         def pair_second(q, h):
-            g = stage.tile([P, 2, P, PACK], BF16, name="w2_grouped", align_bytes=64)
+            g = grouped2.tile([P, 2, P, PACK], BF16, name="w2_grouped", align_bytes=64)
             dst = g[:].rearrange("p e (c i) j -> p e c j i", i=2)
             src = w2_raw[q][:, :, :, h * P : (h + 1) * P].rearrange("p e j (c i) -> p e c j i", i=2)
             if (h, q) in W2_ON_VECTOR:
                 nc.vector.tensor_copy(out=dst, in_=src)
             else:
                 nc.scalar.copy(out=dst, in_=src)
-            wc = codes.tile([P, 2 * P], U32, name="w2_codes", align_bytes=64)
-            ws = codes.tile([P, 2 * P], U8, name="w2_scales", align_bytes=64)
+            wc = codes2.tile([P, 2 * P], U32, name="w2_codes", align_bytes=64)
+            ws = codes2.tile([P, 2 * P], U8, name="w2_scales", align_bytes=64)
             nc.vector.quantize_mx(out=wc[:].bitcast(FP8X4), scales=ws[:], in_=g[:].rearrange("p i c j -> p (i c j)"))
             ps = psum2.tile([P, 2, C], F32, name="ps2")
             for i in range(2):
                 m = slice(i * P, (i + 1) * P)
-                cols = slice(i * C, (i + 1) * C)
+                k = q if q > 1 else 0
+                k = 0 if q < 2 else q - 1
+                e0 = (2 * q if q < 2 else 0) + i
+                cols = slice(e0 * C, (e0 + 1) * C)
                 nc.tensor.matmul_mx(
                     out=ps[:, i, :], lhsT=wc[:, m].bitcast(FP8X4), lhsT_scale=ws[:, m],
-                    rhs=h_codes[q][:, cols].bitcast(FP8X4), rhs_scale=h_scales[q][:, cols], start=True, stop=True,
+                    rhs=h_codes[k][:, cols].bitcast(FP8X4), rhs_scale=h_scales[k][:, cols], start=True, stop=True,
                 )
             nc.scalar.copy(out=y[h][:, 2 * q * C : (2 * q + 2) * C], in_=ps[:].rearrange("p i c -> p (i c)"))
 

from contextlib import ExitStack

import concourse.mybir as mybir

K, T, E, C, H, N = 512, 512, 8, 256, 512, 256
TOP = 4
P = 128
PACK = 4
FLOPS = 2 * E * C * (K * H + H * N)

F32 = mybir.dt.float32
BF16 = mybir.dt.bfloat16
U32 = mybir.dt.uint32
U16 = mybir.dt.uint16
U8 = mybir.dt.uint8
FP8X4 = mybir.dt.float8_e4m3fn_x4
MULT = mybir.AluOpType.mult
ADD = mybir.AluOpType.add
RELU = mybir.ActivationFunctionType.Relu
SQUARE = mybir.ActivationFunctionType.Square

W1_VECTOR = (0, 48, 128, 128, 128, 0, 112, 128)
SQUARE_ON_VECTOR = ()
W2_ON_VECTOR = ((0, 0), (0, 2), (0, 3), (1, 0), (1, 1),)
PIECE = 384


def tile_moe_tk_mlp_relu2_kernel(tc, xT, w1, w2, gate, offs, pos1, pos2, pos3, pos4, out):
    nc = tc.nc
    pos = (pos1, pos2, pos3, pos4)
    with ExitStack() as ctx:
        keep = ctx.enter_context(tc.tile_pool(name="keep", bufs=1))
        stage = ctx.enter_context(tc.tile_pool(name="stage", bufs=2))
        grouped = ctx.enter_context(tc.tile_pool(name="grouped", bufs=3))
        slots_pool = ctx.enter_context(tc.tile_pool(name="slots", bufs=2))
        grouped2 = ctx.enter_context(tc.tile_pool(name="grouped2", bufs=4))
        codes2 = ctx.enter_context(tc.tile_pool(name="codes2", bufs=5))
        sums = ctx.enter_context(tc.tile_pool(name="sums", bufs=1))
        codes = ctx.enter_context(tc.tile_pool(name="codes", bufs=3))
        psum1 = ctx.enter_context(tc.psum_pool(name="psum1", bufs=4))
        psum2 = ctx.enter_context(tc.psum_pool(name="psum2", bufs=4))

        xs = keep.tile([P, T], U8, name="xs", align_bytes=64)
        nc.gpsimd.memset(xs[:], 0)
        x_view = xT.rearrange("(p j) t -> p j t", j=PACK)
        x_raw = []
        for c in range(2):
            t_ = keep.tile([P, PACK, T // 2], F32, name=f"x_raw{c}", align_bytes=64)
            nc.sync.dma_start(out=t_[:], in_=x_view[:, :, c * (T // 2) : (c + 1) * (T // 2)])
            x_raw.append(t_)
        offs_t = keep.tile([P, E * C // 16], U16, name="offs_t")
        nc.sync.dma_start(offs_t[:], offs)
        w1_raw = []
        for e in range(E):
            n_parts = 2 if e == 0 else 1
            parts = []
            for i in range(n_parts):
                width = H // n_parts
                t_ = keep.tile([P, PACK, width], F32, name=f"w1_raw{e}_{i}", align_bytes=64)
                nc.sync.dma_start(out=t_[:], in_=w1[e].rearrange("(p j) c -> p j c", j=PACK)[:, :, i * width : (i + 1) * width])
                parts.append(t_)
            w1_raw.append(parts)
        w2_raw = []
        for q in range(E // 2):
            t_ = keep.tile([P, 2, PACK, N], F32, name=f"w2_raw{q}", align_bytes=64)
            nc.sync.dma_start(out=t_[:], in_=w2[2 * q : 2 * q + 2].rearrange("i (p j) n -> p i j n", j=PACK))
            w2_raw.append(t_)
        pos_t = []
        for r in range(TOP):
            t_ = keep.tile([P, T // 16], U16, name=f"pos_t{r}")
            nc.sync.dma_start(t_[:], pos[r])
            pos_t.append(t_)
        gates = []
        for h in range(2):
            t_ = keep.tile([P, TOP, T], F32, name=f"gates{h}", align_bytes=64)
            nc.sync.dma_start(out=t_[:], in_=gate[:, h * P : (h + 1) * P, :].rearrange("r p t -> p r t"))
            gates.append(t_)

        xw = keep.tile([P, T], U32, name="xw", align_bytes=64)
        for c in range(2):
            xg = keep.tile([P, T // 2, PACK], BF16, name=f"xg{c}", align_bytes=64)
            nc.vector.tensor_copy(
                out=xg[:].rearrange("p (c i) j -> p c j i", i=2),
                in_=x_raw[c][:].rearrange("p j (c i) -> p c j i", i=2),
            )
            cols = slice(c * (T // 2), (c + 1) * (T // 2))
            nc.vector.quantize_mx(out=xw[:, cols].bitcast(FP8X4), scales=xs[:, cols], in_=xg[:].rearrange("p c j -> p (c j)"))

        hb_pair, h_codes, h_scales, pieces, first = [], [], [], [], [0]

        def w1_copy(e):
            g = grouped.tile([P, PACK * H], BF16, name="w1_grouped", align_bytes=64)
            dst = g[:].rearrange("p (t m j) -> p m j t", t=4, j=PACK)
            if e == 0:
                a0, a1 = [t_[:].rearrange("p j (m t) -> p m j t", t=4) for t_ in w1_raw[e]]
                nc.scalar.copy(out=dst[:, : P // 2], in_=a0)
                nc.scalar.copy(out=dst[:, P // 2 :], in_=a1)
                return g
            src = w1_raw[e][0][:].rearrange("p j (m t) -> p m j t", t=4)
            v = W1_VECTOR[e]
            if v < P:
                nc.scalar.copy(out=dst[:, v:], in_=src[:, v:])
            if v > 0:
                nc.vector.tensor_copy(out=dst[:, :v], in_=src[:, :v])
            return g

        def expert_first(e):
            g = w1_copy(e)
            while len(pieces) * PIECE < (e + 1) * C:
                s0 = len(pieces) * PIECE
                s1 = min(s0 + PIECE, E * C)
                xe = slots_pool.tile([P, PIECE], U32, name="xe", align_bytes=64)
                xse = slots_pool.tile([P, PIECE], U8, name="xse", align_bytes=64)
                lst = offs_t[:, s0 // 16 : s1 // 16]
                nc.vector.tensor_copy(xe[:, : s1 - s0], xw[:].indirect(lst))
                nc.vector.tensor_copy(xse[:, : s1 - s0], xs[:].indirect(lst))
                pieces.append((xe, xse))
            wc = codes.tile([P, H], U32, name="w1_codes", align_bytes=64)
            ws = codes.tile([P, H], U8, name="w1_scales", align_bytes=64)
            nc.vector.quantize_mx(out=wc[:].bitcast(FP8X4), scales=ws[:], in_=g[:])
            pos_part = stage.tile([P, C, PACK], F32, name="pos_part", align_bytes=64)
            for b in range(2):
                ps = psum1.tile([P, PACK, P], F32, name="ps1")
                cols = slice(b * P, (b + 1) * P)
                s0 = e * C + b * P
                xe, xse = pieces[s0 // PIECE]
                part = slice(s0 % PIECE, s0 % PIECE + P)
                for t in range(PACK):
                    m = slice(t * P, (t + 1) * P)
                    nc.tensor.matmul_mx(
                        out=ps[:, t, :], lhsT=wc[:, m].bitcast(FP8X4), lhsT_scale=ws[:, m],
                        rhs=xe[:, part].bitcast(FP8X4), rhs_scale=xse[:, part], start=True, stop=True,
                    )
                nc.scalar.activation(pos_part[:, cols, :], ps[:].rearrange("p t n -> p n t"), RELU)
            if e in (0, 4, 6):
                n = 4 if e == 0 else 2
                first[0] = e
                hb_pair.append(keep.tile([P, n * C * PACK], BF16, name=f"hb{e}", align_bytes=64))
                h_codes.append(keep.tile([P, n * C], U32, name=f"h_codes{e}", align_bytes=64))
                h_scales.append(keep.tile([P, n * C], U8, name=f"h_scales{e}", align_bytes=64))
            i = e - first[0]
            hb = hb_pair[-1][:, i * C * PACK : (i + 1) * C * PACK]
            flat = pos_part[:].rearrange("p n t -> p (n t)")
            if e in SQUARE_ON_VECTOR:
                nc.vector.tensor_tensor(hb, flat, flat, MULT)
            else:
                nc.scalar.activation(hb, flat, SQUARE)
            if e >= 6:
                cols, src = slice(i * C, (i + 1) * C), hb
            elif e in (3, 5):
                cols, src = slice(0, (i + 1) * C), hb_pair[-1][:]
            else:
                return
            nc.vector.quantize_mx(out=h_codes[-1][:, cols].bitcast(FP8X4), scales=h_scales[-1][:, cols], in_=src)

        y = [keep.tile([P, E * C], F32, name=f"y{h}") for h in range(2)]

        def pair_second(q, h):
            g = grouped2.tile([P, 2, P, PACK], BF16, name="w2_grouped", align_bytes=64)
            dst = g[:].rearrange("p e (c i) j -> p e c j i", i=2)
            src = w2_raw[q][:, :, :, h * P : (h + 1) * P].rearrange("p e j (c i) -> p e c j i", i=2)
            if (h, q) in W2_ON_VECTOR:
                nc.vector.tensor_copy(out=dst, in_=src)
            else:
                nc.scalar.copy(out=dst, in_=src)
            wc = codes2.tile([P, 2 * P], U32, name="w2_codes", align_bytes=64)
            ws = codes2.tile([P, 2 * P], U8, name="w2_scales", align_bytes=64)
            nc.vector.quantize_mx(out=wc[:].bitcast(FP8X4), scales=ws[:], in_=g[:].rearrange("p i c j -> p (i c j)"))
            ps = psum2.tile([P, 2, C], F32, name="ps2")
            for i in range(2):
                m = slice(i * P, (i + 1) * P)
                k = q if q > 1 else 0
                k = 0 if q < 2 else q - 1
                e0 = (2 * q if q < 2 else 0) + i
                cols = slice(e0 * C, (e0 + 1) * C)
                nc.tensor.matmul_mx(
                    out=ps[:, i, :], lhsT=wc[:, m].bitcast(FP8X4), lhsT_scale=ws[:, m],
                    rhs=h_codes[k][:, cols].bitcast(FP8X4), rhs_scale=h_scales[k][:, cols], start=True, stop=True,
                )
            nc.scalar.copy(out=y[h][:, 2 * q * C : (2 * q + 2) * C], in_=ps[:].rearrange("p i c -> p (i c)"))

        def combine(h):
            prod = [sums.tile([P, T], F32, name=f"prod{r}") for r in range(TOP)]

            def fetch(r, t0, t1):
                nc.vector.tensor_tensor(
                    prod[r][:, t0:t1], y[h][:].indirect(pos_t[r][:, t0 // 16 : t1 // 16]), gates[h][:, r, t0:t1], MULT
                )

            s01 = sums.tile([P, T], F32, name="s01")
            s23 = sums.tile([P, T], F32, name="s23")
            res = sums.tile([P, T], F32, name="res")
            for r in range(TOP):
                fetch(r, 0, T)
            nc.vector.tensor_tensor(s01[:], prod[0][:], prod[1][:], ADD)
            halves = [slice(c * (T // 2), (c + 1) * (T // 2)) for c in range(2)]
            for cols in halves:
                nc.vector.tensor_tensor(s23[:, cols], prod[2][:, cols], prod[3][:, cols], ADD)
            for cols in halves:
                nc.vector.tensor_tensor(res[:, cols], s01[:, cols], s23[:, cols], ADD)
                nc.sync.dma_start(out[h * P : (h + 1) * P, cols], res[:, cols])

        early = {0: 6, 1: 7, 2: 7}
        for e in range(E):
            expert_first(e)
            for q in early:
                if early[q] == e:
                    pair_second(q, 0)
        for h in range(2):
            for q in range(E // 2):
                if h == 1 or q not in early:
                    pair_second(q, h)
        for h in range(2):
            combine(h)
